import numpy as np, ml_dtypes
CORES = [2,3,6,7,58,59,62,63,114,115,118,119]
N = 12
TK = 512
WID = [64,192,512,512,320,320,128,512,256,128,384,64]
def setup_inputs(rng):
    return {"x": rng.standard_normal((N, 128, TK), dtype=np.float32).astype(ml_dtypes.bfloat16), "w": rng.standard_normal((N, 128, 128), dtype=np.float32).astype(ml_dtypes.bfloat16)}
def setup_inputs_big(rng):
    d = setup_inputs(rng)
    for k in ("x", "w"): d[k] = (d[k].astype(np.float32) * 1024.0).astype(d[k].dtype)
    return d
def setup_inputs_small(rng):
    d = setup_inputs(rng)
    for k in ("x", "w"): d[k] = (d[k].astype(np.float32) * (1 / 1024.0)).astype(d[k].dtype)
    return d
def setup_inputs_apart(rng):
    d = setup_inputs(rng)
    f = (10.0 ** rng.permutation(np.linspace(-1.5, 1.5, N))).astype(np.float32).reshape(N, 1, 1)
    for k in ("x", "w"): d[k] = (d[k].astype(np.float32) * f).astype(d[k].dtype)
    return d
def setup_inputs_neg(rng):
    d = setup_inputs(rng)
    d["x"] = (np.abs(d["x"].astype(np.float32)) * 1048576.0).astype(d["x"].dtype); d["w"] = (-np.abs(d["w"].astype(np.float32))).astype(d["w"].dtype)
    return d
def whole(x, w):
    X, W = x.astype(np.float64), w.astype(np.float64)
    y = np.stack([np.max([W[j].T @ X[r] for j in range(N)], axis=0) for r in range(N)])
    return {"y": y.astype(ml_dtypes.bfloat16)}
def reference(x, w):
    o = whole(x, w)["y"].copy()
    for r in range(N):
        o[r][:, WID[r]:] = np.nan
    return {"y": o}

@@ -1,0 +1,148 @@
+from concourse.bass import DstId, RemoteDMATransfer
+from concourse.mybir import AluOpType
+
+N = 12
+M = 128
+TK = 512
+NBANK = 8
+
+CAP = 4
+WEIGHTED = True
+
+SCRATCH = {
+    "wall": ("sbuf", [128, N * M], "bfloat16"),
+    "xs": ("sbuf", [128, TK], "bfloat16"),
+    "acc": ("sbuf", [128, TK], "bfloat16"),
+}
+for _b in range(NBANK):
+    SCRATCH["ps%d" % _b] = ("psum", [128, TK], "float32")
+
+SEMAPHORES = ["wl", "xl", "md", "vd", "st", "sent"] + ["a%d" % j for j in range(N)] + ["f%d" % j for j in range(N)]
+
+
+def _bits(mask):
+    return [b for b in range(mask.bit_length()) if (mask >> b) & 1]
+
+
+def _mask(bs):
+    m = 0
+    for b in bs:
+        m |= 1 << b
+    return m
+
+
+def plan(T, topo):
+    cores = list(T.cores)
+    wid = list(T.tables["WID"])
+    chips = sorted({topo.chip(c) for c in cores})
+    mem = {ch: [r for r in range(N) if topo.chip(cores[r]) == ch] for ch in chips}
+    recv, slot, group = {}, {}, {}
+    for ch in chips:
+        outs = [j for j in range(N) if j not in mem[ch]]
+        quota = {r: 0 for r in mem[ch]}
+        if WEIGHTED:
+            for _ in outs:
+                r = max((r for r in mem[ch] if quota[r] < CAP),
+                        key=lambda r: ((len(outs) - quota[r]) * wid[r], -r))
+                quota[r] += 1
+        else:
+            for i in range(len(outs)):
+                quota[mem[ch][i % len(mem[ch])]] += 1
+        seats = sorted((topo.die(cores[r]), r) for r in mem[ch] for _ in range(quota[r]))
+        srcs = sorted((topo.die(cores[j]), j % len(mem[ch]), j) for j in outs)
+        recv[ch] = {s[2]: seat[1] for s, seat in zip(srcs, seats)}
+        group[ch] = {r: sorted(j for j in outs if recv[ch][j] == r) for r in mem[ch]}
+        order = list(mem[ch])
+        for r in mem[ch]:
+            order += group[ch][r]
+        slot[ch] = {j: i for i, j in enumerate(order)}
+    return cores, wid, chips, mem, recv, slot, group
+
+
+def rank_program(g, core, T, topo):
+    rank = T.rank_of(core)
+    if rank is None:
+        return
+    cores, wid, chips, mem, recv, slot, group = plan(T, topo)
+    ch = topo.chip(core)
+    W = wid[rank]
+    sl = slot[ch]
+    peers = [r for r in mem[ch] if r != rank]
+    peers.sort(key=lambda r: (topo.die(cores[r]) != topo.die(core), r))
+    sem = T.sem
+
+    def wcols(s, n=1):
+        return T.wall[:, s * M:(s + n) * M]
+
+    def dst_id(r):
+        rid, pid, _ = topo.addr(cores[r])
+        return DstId(rid=rid, pnc=pid)
+
+    far = [c for c in cores if topo.chip(c) != ch]
+    near = [cores[r] for r in peers]
+    eng_off = _bits(topo.mask(core, far[0]))
+    eng_all = _bits(topo.mask(core, near[0]))
+    eng_on = [b for b in eng_all if b not in eng_off]
+    n_far_chips = len(chips) - 1
+    per = len(eng_off) // n_far_chips
+    while 128 % per:
+        per -= 1
+    A_OFF, A_ON, F_ALL = per, len(eng_on), len(eng_all)
+
+    g.sync.dma_start(wcols(sl[rank]), T.w[:, :]).then_inc(sem.wl, 16)
+    g.scalar.dma_start(T.xs[:, 0:W], T.x[:, 0:W]).then_inc(sem.xl, 16)
+
+    sent = 0
+    g.wait_ge(sem.wl, 16)
+    trs = []
+    for i, ch2 in enumerate(c for c in chips if c != ch):
+        r2 = recv[ch2][rank]
+        assert topo.may_write(core, cores[r2])
+        trs.append(RemoteDMATransfer(dst_ids=[dst_id(r2)], dma_engine_mask=_mask(eng_off[i * per:(i + 1) * per]),
+                                     remote_sem=sem["a%d" % rank], src=wcols(sl[rank]),
+                                     dst=wcols(slot[ch2][rank])))
+        sent += per
+    g.remote_dma_fused(trs, local_sem=sem.sent)
+    g.remote_dma_fused([RemoteDMATransfer(dst_ids=[dst_id(r) for r in peers], dma_engine_mask=_mask(eng_on),
+                                          remote_sem=sem["a%d" % rank], srcs=[wcols(sl[rank])],
+                                          dsts=[wcols(sl[rank]) for _ in peers])], local_sem=sem.sent)
+    sent += len(eng_on)
+    mine = group[ch][rank]
+    if mine:
+        for j in mine:
+            g.wait_ge(sem["a%d" % j], A_OFF)
+        blk = wcols(sl[mine[0]], len(mine))
+        g.remote_dma_fused([RemoteDMATransfer(dst_ids=[dst_id(r) for r in peers], dma_engine_mask=_mask(eng_all),
+                                              remote_sem=sem["f%d" % rank], srcs=[blk],
+                                              dsts=[blk for _ in peers])], local_sem=sem.sent)
+        sent += len(eng_all)
+    g.wait_ge(sem.sent, sent)
+
+    todo = [(rank, None, 0)]
+    todo += [(r, "a%d" % r, A_ON) for r in peers]
+    todo += [(j, "a%d" % j, A_OFF) for j in mine]
+    for r in sorted(peers, key=lambda r: (len(group[ch][r]), topo.die(cores[r]) != topo.die(core), r)):
+        todo += [(j, "f%d" % r, F_ALL) for j in group[ch][r]]
+    assert sorted(t[0] for t in todo) == list(range(N))
+
+    g.tensor.wait_ge(sem.wl, 16)
+    g.tensor.wait_ge(sem.xl, 16)
+    for k, (j, s, v) in enumerate(todo):
+        if s is not None:
+            g.tensor.wait_ge(sem[s], v)
+        if k >= NBANK:
+            g.tensor.wait_ge(sem.vd, k - NBANK + 1)
+        g.tensor.matmul(T["ps%d" % (k % NBANK)][:, 0:W], wcols(sl[j]), T.xs[:, 0:W], True, True).then_inc(sem.md, 1)
+
+    for k in range(N):
+        g.vector.wait_ge(sem.md, k + 1)
+        ps = T["ps%d" % (k % NBANK)][:, 0:W]
+        if k == 0:
+            g.vector.tensor_copy(T.acc[:, 0:W], ps).then_inc(sem.vd, 1)
+        else:
+            g.vector.wait_ge(sem.vd, k)
+            g.vector.tensor_tensor(T.acc[:, 0:W], ps, T.acc[:, 0:W], AluOpType.max).then_inc(sem.vd, 1)
+
+    g.sync.wait_ge(sem.vd, N)
+    g.sync.dma_start(T.y[:, 0:W], T.acc[:, 0:W]).then_inc(sem.st, 16)
+    g.sync.wait_ge(sem.st, 16)

@@ -5,9 +5,8 @@ N = 12
 M = 128
 TK = 512
 NBANK = 8
-
-CAP = 4
-WEIGHTED = True
+CAP = 2
+SPLIT = 128
 
 SCRATCH = {
     "wall": ("sbuf", [128, N * M], "bfloat16"),
@@ -17,7 +16,7 @@ SCRATCH = {
 for _b in range(NBANK):
     SCRATCH["ps%d" % _b] = ("psum", [128, TK], "float32")
 
-SEMAPHORES = ["wl", "xl", "md", "vd", "st", "sent"] + ["a%d" % j for j in range(N)] + ["f%d" % j for j in range(N)]
+SEMAPHORES = ["wl", "xl", "md", "vd0", "vd1", "st", "sent"] + ["a%d" % j for j in range(N)] + ["f%d" % j for j in range(N)]
 
 
 def _bits(mask):
@@ -40,14 +39,10 @@ def plan(T, topo):
     for ch in chips:
         outs = [j for j in range(N) if j not in mem[ch]]
         quota = {r: 0 for r in mem[ch]}
-        if WEIGHTED:
-            for _ in outs:
-                r = max((r for r in mem[ch] if quota[r] < CAP),
-                        key=lambda r: ((len(outs) - quota[r]) * wid[r], -r))
-                quota[r] += 1
-        else:
-            for i in range(len(outs)):
-                quota[mem[ch][i % len(mem[ch])]] += 1
+        for _ in outs:
+            r = max((r for r in mem[ch] if quota[r] < CAP),
+                    key=lambda r: ((len(outs) - quota[r]) * wid[r], -r))
+            quota[r] += 1
         seats = sorted((topo.die(cores[r]), r) for r in mem[ch] for _ in range(quota[r]))
         srcs = sorted((topo.die(cores[j]), j % len(mem[ch]), j) for j in outs)
         recv[ch] = {s[2]: seat[1] for s, seat in zip(srcs, seats)}
@@ -68,7 +63,10 @@ def rank_program(g, core, T, topo):
     W = wid[rank]
     sl = slot[ch]
     peers = [r for r in mem[ch] if r != rank]
-    peers.sort(key=lambda r: (topo.die(cores[r]) != topo.die(core), r))
+    peers.sort(key=lambda r: (-wid[r], topo.die(cores[r]) != topo.die(core), r))
+    top = max(wid[r] for r in peers)
+    waves = [[r for r in peers if 5 * wid[r] >= 4 * top], [r for r in peers if 5 * wid[r] < 4 * top]]
+    waves = [wv for wv in waves if wv]
     sem = T.sem
 
     def wcols(s, n=1):
@@ -103,19 +101,21 @@ def rank_program(g, core, T, topo):
                                      dst=wcols(slot[ch2][rank])))
         sent += per
     g.remote_dma_fused(trs, local_sem=sem.sent)
-    g.remote_dma_fused([RemoteDMATransfer(dst_ids=[dst_id(r) for r in peers], dma_engine_mask=_mask(eng_on),
-                                          remote_sem=sem["a%d" % rank], srcs=[wcols(sl[rank])],
-                                          dsts=[wcols(sl[rank]) for _ in peers])], local_sem=sem.sent)
-    sent += len(eng_on)
+    for wv in waves:
+        g.remote_dma_fused([RemoteDMATransfer(dst_ids=[dst_id(r) for r in wv], dma_engine_mask=_mask(eng_on),
+                                              remote_sem=sem["a%d" % rank], srcs=[wcols(sl[rank])],
+                                              dsts=[wcols(sl[rank]) for _ in wv])], local_sem=sem.sent)
+        sent += len(eng_on)
     mine = group[ch][rank]
     if mine:
         for j in mine:
             g.wait_ge(sem["a%d" % j], A_OFF)
         blk = wcols(sl[mine[0]], len(mine))
-        g.remote_dma_fused([RemoteDMATransfer(dst_ids=[dst_id(r) for r in peers], dma_engine_mask=_mask(eng_all),
-                                              remote_sem=sem["f%d" % rank], srcs=[blk],
-                                              dsts=[blk for _ in peers])], local_sem=sem.sent)
-        sent += len(eng_all)
+        for wv in waves:
+            g.remote_dma_fused([RemoteDMATransfer(dst_ids=[dst_id(r) for r in wv], dma_engine_mask=_mask(eng_all),
+                                                  remote_sem=sem["f%d" % rank], srcs=[blk],
+                                                  dsts=[blk for _ in wv])], local_sem=sem.sent)
+            sent += len(eng_all)
     g.wait_ge(sem.sent, sent)
 
     todo = [(rank, None, 0)]
@@ -125,24 +125,34 @@ def rank_program(g, core, T, topo):
         todo += [(j, "f%d" % r, F_ALL) for j in group[ch][r]]
     assert sorted(t[0] for t in todo) == list(range(N))
 
+    nh = 2 if W >= SPLIT else 1
+    H = W // nh
+    halves = [(h * H, (h + 1) * H) for h in range(nh)]
+    vds = [sem.vd0, sem.vd1]
+    depth = NBANK // nh
+
     g.tensor.wait_ge(sem.wl, 16)
     g.tensor.wait_ge(sem.xl, 16)
     for k, (j, s, v) in enumerate(todo):
         if s is not None:
             g.tensor.wait_ge(sem[s], v)
-        if k >= NBANK:
-            g.tensor.wait_ge(sem.vd, k - NBANK + 1)
-        g.tensor.matmul(T["ps%d" % (k % NBANK)][:, 0:W], wcols(sl[j]), T.xs[:, 0:W], True, True).then_inc(sem.md, 1)
+        for h, (c0, c1) in enumerate(halves):
+            if k >= depth:
+                g.tensor.wait_ge(vds[h], k - depth + 1)
+            g.tensor.matmul(T["ps%d" % ((k * nh + h) % NBANK)][:, 0:H], wcols(sl[j]), T.xs[:, c0:c1],
+                            True, True).then_inc(sem.md, 1)
 
     for k in range(N):
-        g.vector.wait_ge(sem.md, k + 1)
-        ps = T["ps%d" % (k % NBANK)][:, 0:W]
-        if k == 0:
-            g.vector.tensor_copy(T.acc[:, 0:W], ps).then_inc(sem.vd, 1)
-        else:
-            g.vector.wait_ge(sem.vd, k)
-            g.vector.tensor_tensor(T.acc[:, 0:W], ps, T.acc[:, 0:W], AluOpType.max).then_inc(sem.vd, 1)
+        for h, (c0, c1) in enumerate(halves):
+            g.vector.wait_ge(sem.md, k * nh + h + 1)
+            ps = T["ps%d" % ((k * nh + h) % NBANK)][:, 0:H]
+            if k == 0:
+                g.vector.tensor_copy(T.acc[:, c0:c1], ps).then_inc(vds[h], 1)
+            else:
+                g.vector.wait_ge(vds[h], k)
+                g.vector.tensor_tensor(T.acc[:, c0:c1], ps, T.acc[:, c0:c1], AluOpType.max).then_inc(vds[h], 1)
 
-    g.sync.wait_ge(sem.vd, N)
+    for h in range(nh):
+        g.sync.wait_ge(vds[h], N)
     g.sync.dma_start(T.y[:, 0:W], T.acc[:, 0:W]).then_inc(sem.st, 16)
     g.sync.wait_ge(sem.st, 16)

from concourse.bass import DstId, RemoteDMATransfer
from concourse.mybir import AluOpType

N = 12
M = 128
TK = 512
NBANK = 8
CAP = 2
SPLIT = 128

SCRATCH = {
    "wall": ("sbuf", [128, N * M], "bfloat16"),
    "xs": ("sbuf", [128, TK], "bfloat16"),
    "acc": ("sbuf", [128, TK], "bfloat16"),
}
for _b in range(NBANK):
    SCRATCH["ps%d" % _b] = ("psum", [128, TK], "float32")

SEMAPHORES = ["wl", "xl", "md", "vd0", "vd1", "st", "sent"] + ["a%d" % j for j in range(N)] + ["f%d" % j for j in range(N)]


def _bits(mask):
    return [b for b in range(mask.bit_length()) if (mask >> b) & 1]


def _mask(bs):
    m = 0
    for b in bs:
        m |= 1 << b
    return m


def plan(T, topo):
    cores = list(T.cores)
    wid = list(T.tables["WID"])
    chips = sorted({topo.chip(c) for c in cores})
    mem = {ch: [r for r in range(N) if topo.chip(cores[r]) == ch] for ch in chips}
    recv, slot, group = {}, {}, {}
    for ch in chips:
        outs = [j for j in range(N) if j not in mem[ch]]
        quota = {r: 0 for r in mem[ch]}
        for _ in outs:
            r = max((r for r in mem[ch] if quota[r] < CAP),
                    key=lambda r: ((len(outs) - quota[r]) * wid[r], -r))
            quota[r] += 1
        seats = sorted((topo.die(cores[r]), r) for r in mem[ch] for _ in range(quota[r]))
        srcs = sorted((topo.die(cores[j]), j % len(mem[ch]), j) for j in outs)
        recv[ch] = {s[2]: seat[1] for s, seat in zip(srcs, seats)}
        group[ch] = {r: sorted(j for j in outs if recv[ch][j] == r) for r in mem[ch]}
        order = list(mem[ch])
        for r in mem[ch]:
            order += group[ch][r]
        slot[ch] = {j: i for i, j in enumerate(order)}
    return cores, wid, chips, mem, recv, slot, group


def rank_program(g, core, T, topo):
    rank = T.rank_of(core)
    if rank is None:
        return
    cores, wid, chips, mem, recv, slot, group = plan(T, topo)
    ch = topo.chip(core)
    W = wid[rank]
    sl = slot[ch]
    peers = [r for r in mem[ch] if r != rank]
    peers.sort(key=lambda r: (-wid[r], topo.die(cores[r]) != topo.die(core), r))
    top = max(wid[r] for r in peers)
    waves = [[r for r in peers if 5 * wid[r] >= 4 * top], [r for r in peers if 5 * wid[r] < 4 * top]]
    waves = [wv for wv in waves if wv]
    sem = T.sem

    def wcols(s, n=1):
        return T.wall[:, s * M:(s + n) * M]

    def dst_id(r):
        rid, pid, _ = topo.addr(cores[r])
        return DstId(rid=rid, pnc=pid)

    far = [c for c in cores if topo.chip(c) != ch]
    near = [cores[r] for r in peers]
    eng_off = _bits(topo.mask(core, far[0]))
    eng_all = _bits(topo.mask(core, near[0]))
    eng_on = [b for b in eng_all if b not in eng_off]
    n_far_chips = len(chips) - 1
    per = len(eng_off) // n_far_chips
    while 128 % per:
        per -= 1
    A_OFF, A_ON, F_ALL = per, len(eng_on), len(eng_all)

    g.sync.dma_start(wcols(sl[rank]), T.w[:, :]).then_inc(sem.wl, 16)
    g.scalar.dma_start(T.xs[:, 0:W], T.x[:, 0:W]).then_inc(sem.xl, 16)

    sent = 0
    g.wait_ge(sem.wl, 16)
    trs = []
    for i, ch2 in enumerate(c for c in chips if c != ch):
        r2 = recv[ch2][rank]
        assert topo.may_write(core, cores[r2])
        trs.append(RemoteDMATransfer(dst_ids=[dst_id(r2)], dma_engine_mask=_mask(eng_off[i * per:(i + 1) * per]),
                                     remote_sem=sem["a%d" % rank], src=wcols(sl[rank]),
                                     dst=wcols(slot[ch2][rank])))
        sent += per
    g.remote_dma_fused(trs, local_sem=sem.sent)
    for wv in waves:
        g.remote_dma_fused([RemoteDMATransfer(dst_ids=[dst_id(r) for r in wv], dma_engine_mask=_mask(eng_on),
                                              remote_sem=sem["a%d" % rank], srcs=[wcols(sl[rank])],
                                              dsts=[wcols(sl[rank]) for _ in wv])], local_sem=sem.sent)
        sent += len(eng_on)
    mine = group[ch][rank]
    if mine:
        for j in mine:
            g.wait_ge(sem["a%d" % j], A_OFF)
        blk = wcols(sl[mine[0]], len(mine))
        for wv in waves:
            g.remote_dma_fused([RemoteDMATransfer(dst_ids=[dst_id(r) for r in wv], dma_engine_mask=_mask(eng_all),
                                                  remote_sem=sem["f%d" % rank], srcs=[blk],
                                                  dsts=[blk for _ in wv])], local_sem=sem.sent)
            sent += len(eng_all)
    g.wait_ge(sem.sent, sent)

    todo = [(rank, None, 0)]
    todo += [(r, "a%d" % r, A_ON) for r in peers]
    todo += [(j, "a%d" % j, A_OFF) for j in mine]
    for r in sorted(peers, key=lambda r: (len(group[ch][r]), topo.die(cores[r]) != topo.die(core), r)):
        todo += [(j, "f%d" % r, F_ALL) for j in group[ch][r]]
    assert sorted(t[0] for t in todo) == list(range(N))

    nh = 2 if W >= SPLIT else 1
    H = W // nh
    halves = [(h * H, (h + 1) * H) for h in range(nh)]
    vds = [sem.vd0, sem.vd1]
    depth = NBANK // nh

    g.tensor.wait_ge(sem.wl, 16)
    g.tensor.wait_ge(sem.xl, 16)
    for k, (j, s, v) in enumerate(todo):
        if s is not None:
            g.tensor.wait_ge(sem[s], v)
        for h, (c0, c1) in enumerate(halves):
            if k >= depth:
                g.tensor.wait_ge(vds[h], k - depth + 1)
            g.tensor.matmul(T["ps%d" % ((k * nh + h) % NBANK)][:, 0:H], wcols(sl[j]), T.xs[:, c0:c1],
                            True, True).then_inc(sem.md, 1)

    for k in range(N):
        for h, (c0, c1) in enumerate(halves):
            g.vector.wait_ge(sem.md, k * nh + h + 1)
            ps = T["ps%d" % ((k * nh + h) % NBANK)][:, 0:H]
            if k == 0:
                g.vector.tensor_copy(T.acc[:, c0:c1], ps).then_inc(vds[h], 1)
            else:
                g.vector.wait_ge(vds[h], k)
                g.vector.tensor_tensor(T.acc[:, c0:c1], ps, T.acc[:, c0:c1], AluOpType.max).then_inc(vds[h], 1)

    for h in range(nh):
        g.sync.wait_ge(vds[h], N)
    g.sync.dma_start(T.y[:, 0:W], T.acc[:, 0:W]).then_inc(sem.st, 16)
    g.sync.wait_ge(sem.st, 16)
